import numpy as np
import ml_dtypes


def mxq(x, axis, fmt="e4m3"):
    dtype, down = {"e4m3": (ml_dtypes.float8_e4m3fn, 7), "e5m2": (ml_dtypes.float8_e5m2, 14)}[fmt]
    v = np.moveaxis(np.asarray(x, np.float32).astype(ml_dtypes.bfloat16).astype(np.float64), axis, -1)
    blocks = v.reshape(v.shape[:-1] + (-1, 32))
    amax = np.abs(blocks).max(-1, keepdims=True)
    byte = np.maximum(np.where(amax > 0, np.frexp(amax)[1] - 1 + 127, 0) - down, 1)
    scale = np.exp2(byte - 127.0)
    codes = (blocks / scale).astype(np.float32).astype(dtype).astype(np.float64)
    return np.moveaxis((codes * scale).reshape(v.shape), -1, axis)


WIDE = False


def mx_kscale(k, group=512):
    if not WIDE:
        return np.ones(k)
    levels = np.array([18, -18])
    if group != 512:
        return np.exp2(np.random.permutation(np.resize(levels, k // group))).repeat(group)
    if k % 512:
        return np.exp2(np.random.permutation(np.resize(levels, k // 32))).repeat(32)
    a = np.empty((k // 512, 16))
    for p in range(k // 512):
        a[p, :8] = np.random.permutation(np.resize(levels, 8))
        for g in range(8):
            far = levels[np.abs(levels - a[p, g]) >= 10]
            a[p, g + 8] = far[np.random.randint(len(far))]
    return np.exp2(a.ravel()).repeat(32)


def f64(x):
    return np.asarray(x).astype(np.float64)


def sigmoid(v):
    return 1.0 / (1.0 + np.exp(-v))


G, D, M, O, N = 4, 128, 128, 128, 512


def sgn(shape):
    return np.random.uniform(0.5, 2.0, shape) * np.where(np.random.standard_normal(shape) < 0, -1.0, 1.0)


def setup_inputs():
    n = np.random.standard_normal
    s_d = mx_kscale(D, 0)
    s_m = mx_kscale(M, 0)
    return {
        "x": (n((G, D, N)) * s_d[:, None]).astype(np.float32),
        "w1": (n((G, D, M)) / np.sqrt(D) / s_d[:, None]).astype(np.float32),
        "w2": (n((G, D, M)) / np.sqrt(D) / s_d[:, None]).astype(np.float32),
        "gn": (np.random.uniform(0.5, 2.0, (G, M, 1))).astype(np.float32),
        "hs": (sgn((G, M, 1)) * s_m[:, None]).astype(np.float32),
        "wo2": (n((G, M, O)) / np.sqrt(M) / s_m[:, None]).astype(np.float32),
        "res": (0.5 * n((G, O, N))).astype(np.float32),
    }


def reference(x, w1, w2, gn, hs, wo2, res):
    w1q = mxq(f64(w1), 1, "e4m3")
    xq = mxq(f64(x), 1, "e4m3")
    z1 = w1q.transpose(0, 2, 1) @ xq
    w2q = mxq(f64(w2), 1, "e4m3")
    z2 = w2q.transpose(0, 2, 1) @ xq
    rm = np.sqrt(np.mean(np.square(z1), axis=-1, keepdims=True) + 0.01)
    nz = z1 / rm * f64(gn)
    h = nz * sigmoid(z2)
    hh = h * f64(hs)
    wo2q = mxq(f64(wo2), 1, "e4m3")
    hhq = mxq(hh, 1, "e4m3")
    y0 = wo2q.transpose(0, 2, 1) @ hhq
    y = y0 + f64(res)
    return y

@@ -1,0 +1,184 @@
+from contextlib import ExitStack
+
+import concourse.mybir as mybir
+
+G, D, M, O, N = 4, 128, 128, 128, 512
+FLOPS = 3 * 2 * G * D * M * N
+
+F32 = mybir.dt.float32
+BF16 = mybir.dt.bfloat16
+U32 = mybir.dt.uint32
+U8 = mybir.dt.uint8
+FP8X4 = mybir.dt.float8_e4m3fn_x4
+ACT = mybir.ActivationFunctionType
+ALU = mybir.AluOpType
+
+P = 128
+PACK = 4
+ROWS = 32
+HALF = N // 2
+CALL = 128
+EPS = 0.01
+VECTOR_COLS = 176
+
+
+def tile_rows_frownorm_kernel(tc, x, w1, w2, gn, hs, wo2, res, out):
+    nc = tc.nc
+
+    def packed(ap):
+        return ap.rearrange("g (p j) n -> (g p) j n", j=PACK)
+
+    def interleave(copy, dst, src, c0, c1):
+        copy(
+            out=dst[:, c0:c1, :].rearrange("p (c i) j -> p c j i", i=4),
+            in_=src[:, :, c0:c1].rearrange("p j (c i) -> p c j i", i=4),
+        )
+
+    with ExitStack() as ctx:
+        sb = ctx.enter_context(tc.tile_pool(name="sb", bufs=1))
+        ps = ctx.enter_context(tc.psum_pool(name="ps", bufs=1))
+        ctx.enter_context(tc.manual_schedule())
+
+        def operand(name, width):
+            words = sb.tile([P, width, PACK], BF16, name=name + "_words", align_bytes=64)
+            codes = sb.tile([P, width], U32, name=name + "_codes", align_bytes=64)
+            scales = sb.tile([P, width], U8, name=name + "_scales", align_bytes=64)
+            return words, codes, scales
+
+        def quantize(op):
+            words, codes, scales = op
+            nc.vector.quantize_mx(
+                out=codes[:].bitcast(FP8X4),
+                scales=scales[:],
+                in_=words[:].rearrange("p n j -> p (n j)"),
+            )
+
+        def product(banks, weights, moving, col0):
+            for c in range(0, HALF, CALL):
+                for g in range(G):
+                    rows = slice(ROWS * g, ROWS * (g + 1))
+                    nc.tensor.matmul_mx(
+                        out=banks[g][:, col0 + c : col0 + c + CALL],
+                        lhsT=weights[1][rows, :].bitcast(FP8X4),
+                        lhsT_scale=weights[2][rows, :],
+                        rhs=moving[1][rows, c : c + CALL].bitcast(FP8X4),
+                        rhs_scale=moving[2][rows, c : c + CALL],
+                        start=True,
+                        stop=True,
+                    )
+
+        halves = [slice(0, HALF), slice(HALF, N)]
+        x_raw = [sb.tile([P, PACK, HALF], F32, name="x_raw%d" % h) for h in range(2)]
+        w1_raw = sb.tile([P, PACK, M], F32)
+        w2_raw = sb.tile([P, PACK, M], F32)
+        wo_raw = sb.tile([P, PACK, O], F32)
+        gn_sb = sb.tile([P, G], F32)
+        hs_sb = sb.tile([P, G], F32)
+        res_sb = sb.tile([P, G, N], F32)
+
+        nc.sync.dma_start(out=x_raw[0][:], in_=packed(x)[:, :, halves[0]])
+        nc.sync.dma_start(out=w1_raw[:], in_=packed(w1))
+        nc.sync.dma_start(out=x_raw[1][:], in_=packed(x)[:, :, halves[1]])
+        nc.sync.dma_start(out=w2_raw[:], in_=packed(w2))
+        with nc.allow_non_contiguous_dma(reason="one factor a partition"):
+            nc.sync.dma_start(out=gn_sb[:], in_=gn.rearrange("g m o -> m (g o)"))
+            nc.sync.dma_start(out=hs_sb[:], in_=hs.rearrange("g m o -> m (g o)"))
+        nc.sync.dma_start(out=wo_raw[:], in_=packed(wo2))
+        nc.sync.dma_start(out=res_sb[:], in_=res.rearrange("g o n -> o g n"))
+
+        minus_half = sb.tile([P, 2], F32)
+        warm = sb.tile([P, 2], F32)
+        nc.gpsimd.memset(minus_half[:], -0.5)
+        nc.scalar.activation(out=warm[:], in_=minus_half[:], func=ACT.Sigmoid)
+
+        xq = [operand("x%d" % h, HALF) for h in range(2)]
+        w1q = operand("w1", M)
+        w2q = operand("w2", M)
+        woq = operand("wo", O)
+        hq = [operand("h%d" % h, HALF) for h in range(2)]
+        bank_a = [ps.tile([P, N], F32, name="bank_a%d" % g) for g in range(G)]
+        bank_b = [ps.tile([P, N], F32, name="bank_b%d" % g) for g in range(G)]
+
+        def shared_interleave(op, raw):
+            interleave(nc.vector.tensor_copy, op[0], raw, 0, VECTOR_COLS)
+            interleave(nc.scalar.copy, op[0], raw, VECTOR_COLS, HALF)
+
+        shared_interleave(xq[0], x_raw[0])
+        interleave(nc.scalar.copy, w1q[0], w1_raw, 0, M)
+        quantize(xq[0])
+        quantize(w1q)
+        product(bank_a, w1q, xq[0], 0)
+        shared_interleave(xq[1], x_raw[1])
+        interleave(nc.scalar.copy, w2q[0], w2_raw, 0, M)
+        quantize(xq[1])
+        product(bank_a, w1q, xq[1], HALF)
+        quantize(w2q)
+        product(bank_b, w2q, xq[0], 0)
+        product(bank_b, w2q, xq[1], HALF)
+
+        gain = sb.tile([P, G], F32)
+        nc.gpsimd.tensor_tensor(out=gain[:], in0=gn_sb[:], in1=hs_sb[:], op=ALU.mult)
+
+        squares = sb.tile([P, N], BF16)
+        sums = sb.tile([P, 2], F32)
+        stats = sb.tile([P, 2, 6], F32)
+        mean_var = sb.tile([P, 2, 2], F32)
+        mean_sq = sb.tile([P, 2], F32)
+        power = [sb.tile([P, 2], F32, name="power%d" % k) for k in range(2)]
+        root = [sb.tile([P, 2], F32, name="root%d" % k) for k in range(2)]
+        factor = [sb.tile([P, 2], F32, name="factor%d" % k) for k in range(2)]
+        for k in range(2):
+            nc.scalar.activation(
+                out=squares[:], in_=bank_a[k][:], func=ACT.Square, accum_out=sums[:, k : k + 1]
+            )
+            nc.vector.bn_stats(out=stats[:, k, :], in_=bank_a[2 + k][:])
+        for k in range(2):
+            nc.vector.bn_aggr(out=mean_var[:, k, :], in_=stats[:, k, :])
+        nc.vector.tensor_tensor(
+            out=mean_sq[:], in0=mean_var[:, :, 0], in1=mean_var[:, :, 0], op=ALU.mult
+        )
+        nc.vector.scalar_tensor_tensor(
+            out=power[1][:], in0=mean_var[:, :, 1], scalar=EPS, in1=mean_sq[:], op0=ALU.add, op1=ALU.add
+        )
+        nc.gpsimd.tensor_scalar(
+            out=power[0][:], in0=sums[:], scalar1=1.0 / N, scalar2=EPS, op0=ALU.mult, op1=ALU.add
+        )
+        for k in range(2):
+            nc.gpsimd.tensor_tensor(out=root[k][:], in0=power[k][:], in1=minus_half[:], op=ALU.pow)
+            nc.gpsimd.tensor_tensor(
+                out=factor[k][:], in0=root[k][:], in1=gain[:, 2 * k : 2 * k + 2], op=ALU.mult
+            )
+
+        h_raw = [sb.tile([P, PACK, HALF], BF16, name="h_raw%d" % h) for h in range(2)]
+        for h in range(2):
+            for g in range(G):
+                gate = sb.tile([P, HALF], F32, name="gate%d_%d" % (h, g))
+                hh = sb.tile([P, HALF], BF16, name="hh%d_%d" % (h, g))
+                nc.scalar.activation(out=gate[:], in_=bank_b[g][:, halves[h]], func=ACT.Sigmoid)
+                nc.vector.scalar_tensor_tensor(
+                    out=hh[:],
+                    in0=bank_a[g][:, halves[h]],
+                    scalar=factor[g // 2][:, g % 2 : g % 2 + 1],
+                    in1=gate[:],
+                    op0=ALU.mult,
+                    op1=ALU.mult,
+                )
+                nc.sync.dma_start(out=h_raw[h][ROWS * g : ROWS * (g + 1), :, :], in_=hh[:])
+
+        interleave(nc.vector.tensor_copy, woq[0], wo_raw, 0, O)
+        shared_interleave(hq[0], h_raw[0])
+        quantize(woq)
+        quantize(hq[0])
+        product(bank_b, woq, hq[0], 0)
+        shared_interleave(hq[1], h_raw[1])
+        quantize(hq[1])
+        product(bank_a, woq, hq[1], 0)
+
+        out_rows = out.rearrange("g o n -> o g n")
+        for h, banks in enumerate((bank_b, bank_a)):
+            for g in range(G):
+                y = sb.tile([P, HALF], F32, name="y%d_%d" % (h, g))
+                nc.vector.tensor_tensor(
+                    out=y[:], in0=banks[g][:, 0:HALF], in1=res_sb[:, g, halves[h]], op=ALU.add
+                )
+                nc.sync.dma_start(out=out_rows[:, g, halves[h]], in_=y[:])

@@ -19,7 +19,6 @@ ROWS = 32
 HALF = N // 2
 CALL = 128
 EPS = 0.01
-VECTOR_COLS = 176
 
 
 def tile_rows_frownorm_kernel(tc, x, w1, w2, gn, hs, wo2, res, out):
@@ -55,14 +54,14 @@ def tile_rows_frownorm_kernel(tc, x, w1, w2, gn, hs, wo2, res, out):
 
         def product(banks, weights, moving, col0):
             for c in range(0, HALF, CALL):
-                for g in range(G):
-                    rows = slice(ROWS * g, ROWS * (g + 1))
+                for g in (0, 2, 1, 3):
+                    tile_rows = slice(ROWS * g, ROWS * (g + 1))
                     nc.tensor.matmul_mx(
                         out=banks[g][:, col0 + c : col0 + c + CALL],
-                        lhsT=weights[1][rows, :].bitcast(FP8X4),
-                        lhsT_scale=weights[2][rows, :],
-                        rhs=moving[1][rows, c : c + CALL].bitcast(FP8X4),
-                        rhs_scale=moving[2][rows, c : c + CALL],
+                        lhsT=weights[1][tile_rows, :].bitcast(FP8X4),
+                        lhsT_scale=weights[2][tile_rows, :],
+                        rhs=moving[1][tile_rows, c : c + CALL].bitcast(FP8X4),
+                        rhs_scale=moving[2][tile_rows, c : c + CALL],
                         start=True,
                         stop=True,
                     )
@@ -72,23 +71,30 @@ def tile_rows_frownorm_kernel(tc, x, w1, w2, gn, hs, wo2, res, out):
         w1_raw = sb.tile([P, PACK, M], F32)
         w2_raw = sb.tile([P, PACK, M], F32)
         wo_raw = sb.tile([P, PACK, O], F32)
-        gn_sb = sb.tile([P, G], F32)
-        hs_sb = sb.tile([P, G], F32)
+        rows = sb.tile([P, 2 * M], F32, align_bytes=64)
+        cols = sb.tile([P, 2 * M], F32, align_bytes=64)
         res_sb = sb.tile([P, G, N], F32)
 
         nc.sync.dma_start(out=x_raw[0][:], in_=packed(x)[:, :, halves[0]])
+        nc.gpsimd.memset(rows[:], 0.0)
+        for k, vec in enumerate((gn, hs)):
+            nc.sync.dma_start(
+                out=rows[0:P:ROWS, k * M : (k + 1) * M].rearrange("q (g c) -> q g c", g=G),
+                in_=vec.rearrange("g (q c) o -> q g (c o)", c=ROWS),
+            )
         nc.sync.dma_start(out=w1_raw[:], in_=packed(w1))
         nc.sync.dma_start(out=x_raw[1][:], in_=packed(x)[:, :, halves[1]])
         nc.sync.dma_start(out=w2_raw[:], in_=packed(w2))
-        with nc.allow_non_contiguous_dma(reason="one factor a partition"):
-            nc.sync.dma_start(out=gn_sb[:], in_=gn.rearrange("g m o -> m (g o)"))
-            nc.sync.dma_start(out=hs_sb[:], in_=hs.rearrange("g m o -> m (g o)"))
         nc.sync.dma_start(out=wo_raw[:], in_=packed(wo2))
         nc.sync.dma_start(out=res_sb[:], in_=res.rearrange("g o n -> o g n"))
 
         minus_half = sb.tile([P, 2], F32)
+        ones = sb.tile([P, 2], F32)
         warm = sb.tile([P, 2], F32)
+        warm_pow = sb.tile([P, 2], F32)
         nc.gpsimd.memset(minus_half[:], -0.5)
+        nc.gpsimd.memset(ones[:], 1.0)
+        nc.gpsimd.tensor_tensor(out=warm_pow[:], in0=ones[:], in1=minus_half[:], op=ALU.pow)
         nc.scalar.activation(out=warm[:], in_=minus_half[:], func=ACT.Sigmoid)
 
         xq = [operand("x%d" % h, HALF) for h in range(2)]
@@ -96,89 +102,119 @@ def tile_rows_frownorm_kernel(tc, x, w1, w2, gn, hs, wo2, res, out):
         w2q = operand("w2", M)
         woq = operand("wo", O)
         hq = [operand("h%d" % h, HALF) for h in range(2)]
-        bank_a = [ps.tile([P, N], F32, name="bank_a%d" % g) for g in range(G)]
-        bank_b = [ps.tile([P, N], F32, name="bank_b%d" % g) for g in range(G)]
+        banks = [[ps.tile([P, N], F32, name="bank%d_%d" % (h, g)) for g in range(G)] for h in range(2)]
+        values = slice(0, HALF)
+        gates = slice(HALF, N)
 
-        def shared_interleave(op, raw):
-            interleave(nc.vector.tensor_copy, op[0], raw, 0, VECTOR_COLS)
-            interleave(nc.scalar.copy, op[0], raw, VECTOR_COLS, HALF)
+        def shared_interleave(op, raw, split):
+            interleave(nc.vector.tensor_copy, op[0], raw, 0, split)
+            interleave(nc.scalar.copy, op[0], raw, split, HALF)
 
-        shared_interleave(xq[0], x_raw[0])
-        interleave(nc.scalar.copy, w1q[0], w1_raw, 0, M)
-        quantize(xq[0])
-        quantize(w1q)
-        product(bank_a, w1q, xq[0], 0)
-        shared_interleave(xq[1], x_raw[1])
-        interleave(nc.scalar.copy, w2q[0], w2_raw, 0, M)
-        quantize(xq[1])
-        product(bank_a, w1q, xq[1], HALF)
-        quantize(w2q)
-        product(bank_b, w2q, xq[0], 0)
-        product(bank_b, w2q, xq[1], HALF)
+        squares = sb.tile([P, 2, 2, HALF], BF16)
+        sums = [sb.tile([P, 2], F32, name="sums%d" % h) for h in range(2)]
+        stats = sb.tile([P, 2, 2, 6], F32)
+
+        def statistics(h, k):
+            nc.scalar.activation(
+                out=squares[:, h, k, :],
+                in_=banks[h][k][:, values],
+                func=ACT.Square,
+                accum_out=sums[h][:, k : k + 1],
+            )
+            nc.vector.bn_stats(out=stats[:, k, h, :], in_=banks[h][2 + k][:, values])
 
         gain = sb.tile([P, G], F32)
-        nc.gpsimd.tensor_tensor(out=gain[:], in0=gn_sb[:], in1=hs_sb[:], op=ALU.mult)
+        first_part = sb.tile([P, 2], F32)
 
-        squares = sb.tile([P, N], BF16)
-        sums = sb.tile([P, 2], F32)
-        stats = sb.tile([P, 2, 6], F32)
+        shared_interleave(xq[0], x_raw[0], 144)
+        interleave(nc.scalar.copy, w1q[0], w1_raw, 0, M)
+        quantize(xq[0])
+        nc.vector.transpose(out=cols[:], in_=rows[:])
+        nc.gpsimd.tensor_tensor(out=gain[:], in0=cols[:, 0:M:ROWS], in1=cols[:, M : 2 * M : ROWS], op=ALU.mult)
+        quantize(w1q)
+        product(banks[0], w1q, xq[0], 0)
+        shared_interleave(xq[1], x_raw[1], 144)
+        interleave(nc.scalar.copy, w2q[0], w2_raw, 0, M)
+        quantize(xq[1])
+        product(banks[1], w1q, xq[1], 0)
+        statistics(0, 0)
+        quantize(w2q)
+        statistics(0, 1)
+        nc.gpsimd.tensor_scalar(
+            out=first_part[:], in0=sums[0][:], scalar1=1.0 / N, scalar2=EPS, op0=ALU.mult, op1=ALU.add
+        )
+        product(banks[0], w2q, xq[0], HALF)
+        statistics(1, 0)
+        statistics(1, 1)
+        product(banks[1], w2q, xq[1], HALF)
+
         mean_var = sb.tile([P, 2, 2], F32)
         mean_sq = sb.tile([P, 2], F32)
         power = [sb.tile([P, 2], F32, name="power%d" % k) for k in range(2)]
         root = [sb.tile([P, 2], F32, name="root%d" % k) for k in range(2)]
         factor = [sb.tile([P, 2], F32, name="factor%d" % k) for k in range(2)]
-        for k in range(2):
-            nc.scalar.activation(
-                out=squares[:], in_=bank_a[k][:], func=ACT.Square, accum_out=sums[:, k : k + 1]
-            )
-            nc.vector.bn_stats(out=stats[:, k, :], in_=bank_a[2 + k][:])
-        for k in range(2):
-            nc.vector.bn_aggr(out=mean_var[:, k, :], in_=stats[:, k, :])
+        nc.vector.bn_aggr(out=mean_var[:, 0, :], in_=stats[:, 0, :, :].rearrange("p h s -> p (h s)"))
+        nc.vector.scalar_tensor_tensor(
+            out=power[0][:], in0=sums[1][:], scalar=1.0 / N, in1=first_part[:], op0=ALU.mult, op1=ALU.add
+        )
+        nc.vector.bn_aggr(out=mean_var[:, 1, :], in_=stats[:, 1, :, :].rearrange("p h s -> p (h s)"))
         nc.vector.tensor_tensor(
             out=mean_sq[:], in0=mean_var[:, :, 0], in1=mean_var[:, :, 0], op=ALU.mult
         )
         nc.vector.scalar_tensor_tensor(
             out=power[1][:], in0=mean_var[:, :, 1], scalar=EPS, in1=mean_sq[:], op0=ALU.add, op1=ALU.add
         )
-        nc.gpsimd.tensor_scalar(
-            out=power[0][:], in0=sums[:], scalar1=1.0 / N, scalar2=EPS, op0=ALU.mult, op1=ALU.add
-        )
         for k in range(2):
             nc.gpsimd.tensor_tensor(out=root[k][:], in0=power[k][:], in1=minus_half[:], op=ALU.pow)
-            nc.gpsimd.tensor_tensor(
+
+        def row_factor(k):
+            nc.vector.tensor_tensor(
                 out=factor[k][:], in0=root[k][:], in1=gain[:, 2 * k : 2 * k + 2], op=ALU.mult
             )
 
         h_raw = [sb.tile([P, PACK, HALF], BF16, name="h_raw%d" % h) for h in range(2)]
-        for h in range(2):
-            for g in range(G):
-                gate = sb.tile([P, HALF], F32, name="gate%d_%d" % (h, g))
-                hh = sb.tile([P, HALF], BF16, name="hh%d_%d" % (h, g))
-                nc.scalar.activation(out=gate[:], in_=bank_b[g][:, halves[h]], func=ACT.Sigmoid)
-                nc.vector.scalar_tensor_tensor(
-                    out=hh[:],
-                    in0=bank_a[g][:, halves[h]],
-                    scalar=factor[g // 2][:, g % 2 : g % 2 + 1],
-                    in1=gate[:],
-                    op0=ALU.mult,
-                    op1=ALU.mult,
-                )
-                nc.sync.dma_start(out=h_raw[h][ROWS * g : ROWS * (g + 1), :, :], in_=hh[:])
 
-        interleave(nc.vector.tensor_copy, woq[0], wo_raw, 0, O)
-        shared_interleave(hq[0], h_raw[0])
-        quantize(woq)
-        quantize(hq[0])
-        product(bank_b, woq, hq[0], 0)
-        shared_interleave(hq[1], h_raw[1])
-        quantize(hq[1])
-        product(bank_a, woq, hq[1], 0)
+        def hidden(h, g):
+            gate = sb.tile([P, HALF], F32, name="gate%d_%d" % (h, g))
+            hh = sb.tile([P, HALF], BF16, name="hh%d_%d" % (h, g))
+            nc.scalar.activation(out=gate[:], in_=banks[h][g][:, gates], func=ACT.Sigmoid)
+            nc.vector.scalar_tensor_tensor(
+                out=hh[:],
+                in0=banks[h][g][:, values],
+                scalar=factor[g // 2][:, g % 2 : g % 2 + 1],
+                in1=gate[:],
+                op0=ALU.mult,
+                op1=ALU.mult,
+            )
+            nc.sync.dma_start(out=h_raw[h][ROWS * g : ROWS * (g + 1), :, :], in_=hh[:])
+
+        row_factor(0)
+        hidden(0, 0)
+        row_factor(1)
+        for g in range(1, G):
+            hidden(0, g)
+        for g in range(G):
+            hidden(1, g)
 
         out_rows = out.rearrange("g o n -> o g n")
-        for h, banks in enumerate((bank_b, bank_a)):
-            for g in range(G):
-                y = sb.tile([P, HALF], F32, name="y%d_%d" % (h, g))
-                nc.vector.tensor_tensor(
-                    out=y[:], in0=banks[g][:, 0:HALF], in1=res_sb[:, g, halves[h]], op=ALU.add
-                )
-                nc.sync.dma_start(out=out_rows[:, g, halves[h]], in_=y[:])
+
+        def finish(h, g):
+            y = sb.tile([P, HALF], F32, name="y%d_%d" % (h, g))
+            nc.vector.tensor_tensor(
+                out=y[:], in0=banks[h][g][:, values], in1=res_sb[:, g, halves[h]], op=ALU.add
+            )
+            nc.sync.dma_start(out=out_rows[:, g, halves[h]], in_=y[:])
+
+        interleave(nc.vector.tensor_copy, woq[0], wo_raw, 0, O)
+        shared_interleave(hq[0], h_raw[0], 176)
+        quantize(woq)
+        quantize(hq[0])
+        product(banks[0], woq, hq[0], 0)
+        shared_interleave(hq[1], h_raw[1], 128)
+        finish(0, 0)
+        quantize(hq[1])
+        product(banks[1], woq, hq[1], 0)
+        for g in (2, 1, 3):
+            finish(0, g)
+        for g in (0, 2, 1, 3):
+            finish(1, g)

@@ -52,9 +52,9 @@ def tile_rows_frownorm_kernel(tc, x, w1, w2, gn, hs, wo2, res, out):
                 in_=words[:].rearrange("p n j -> p (n j)"),
             )
 
-        def product(banks, weights, moving, col0):
+        def product(banks, weights, moving, col0, groups):
             for c in range(0, HALF, CALL):
-                for g in (0, 2, 1, 3):
+                for g in groups:
                     tile_rows = slice(ROWS * g, ROWS * (g + 1))
                     nc.tensor.matmul_mx(
                         out=banks[g][:, col0 + c : col0 + c + CALL],
@@ -75,14 +75,14 @@ def tile_rows_frownorm_kernel(tc, x, w1, w2, gn, hs, wo2, res, out):
         cols = sb.tile([P, 2 * M], F32, align_bytes=64)
         res_sb = sb.tile([P, G, N], F32)
 
-        nc.sync.dma_start(out=x_raw[0][:], in_=packed(x)[:, :, halves[0]])
+        nc.sync.dma_start(out=w1_raw[:], in_=packed(w1))
         nc.gpsimd.memset(rows[:], 0.0)
         for k, vec in enumerate((gn, hs)):
             nc.sync.dma_start(
                 out=rows[0:P:ROWS, k * M : (k + 1) * M].rearrange("q (g c) -> q g c", g=G),
                 in_=vec.rearrange("g (q c) o -> q g (c o)", c=ROWS),
             )
-        nc.sync.dma_start(out=w1_raw[:], in_=packed(w1))
+        nc.sync.dma_start(out=x_raw[0][:], in_=packed(x)[:, :, halves[0]])
         nc.sync.dma_start(out=x_raw[1][:], in_=packed(x)[:, :, halves[1]])
         nc.sync.dma_start(out=w2_raw[:], in_=packed(w2))
         nc.sync.dma_start(out=wo_raw[:], in_=packed(wo2))
@@ -114,87 +114,125 @@ def tile_rows_frownorm_kernel(tc, x, w1, w2, gn, hs, wo2, res, out):
         sums = [sb.tile([P, 2], F32, name="sums%d" % h) for h in range(2)]
         stats = sb.tile([P, 2, 2, 6], F32)
 
-        def statistics(h, k):
+        def sum_squares(h, k):
             nc.scalar.activation(
                 out=squares[:, h, k, :],
                 in_=banks[h][k][:, values],
                 func=ACT.Square,
                 accum_out=sums[h][:, k : k + 1],
             )
+
+        def moments(h, k):
             nc.vector.bn_stats(out=stats[:, k, h, :], in_=banks[h][2 + k][:, values])
 
         gain = sb.tile([P, G], F32)
         first_part = sb.tile([P, 2], F32)
-
-        shared_interleave(xq[0], x_raw[0], 144)
-        interleave(nc.scalar.copy, w1q[0], w1_raw, 0, M)
-        quantize(xq[0])
-        nc.vector.transpose(out=cols[:], in_=rows[:])
-        nc.gpsimd.tensor_tensor(out=gain[:], in0=cols[:, 0:M:ROWS], in1=cols[:, M : 2 * M : ROWS], op=ALU.mult)
-        quantize(w1q)
-        product(banks[0], w1q, xq[0], 0)
-        shared_interleave(xq[1], x_raw[1], 144)
-        interleave(nc.scalar.copy, w2q[0], w2_raw, 0, M)
-        quantize(xq[1])
-        product(banks[1], w1q, xq[1], 0)
-        statistics(0, 0)
-        quantize(w2q)
-        statistics(0, 1)
-        nc.gpsimd.tensor_scalar(
-            out=first_part[:], in0=sums[0][:], scalar1=1.0 / N, scalar2=EPS, op0=ALU.mult, op1=ALU.add
-        )
-        product(banks[0], w2q, xq[0], HALF)
-        statistics(1, 0)
-        statistics(1, 1)
-        product(banks[1], w2q, xq[1], HALF)
-
         mean_var = sb.tile([P, 2, 2], F32)
-        mean_sq = sb.tile([P, 2], F32)
-        power = [sb.tile([P, 2], F32, name="power%d" % k) for k in range(2)]
-        root = [sb.tile([P, 2], F32, name="root%d" % k) for k in range(2)]
-        factor = [sb.tile([P, 2], F32, name="factor%d" % k) for k in range(2)]
-        nc.vector.bn_aggr(out=mean_var[:, 0, :], in_=stats[:, 0, :, :].rearrange("p h s -> p (h s)"))
-        nc.vector.scalar_tensor_tensor(
-            out=power[0][:], in0=sums[1][:], scalar=1.0 / N, in1=first_part[:], op0=ALU.mult, op1=ALU.add
-        )
-        nc.vector.bn_aggr(out=mean_var[:, 1, :], in_=stats[:, 1, :, :].rearrange("p h s -> p (h s)"))
-        nc.vector.tensor_tensor(
-            out=mean_sq[:], in0=mean_var[:, :, 0], in1=mean_var[:, :, 0], op=ALU.mult
-        )
-        nc.vector.scalar_tensor_tensor(
-            out=power[1][:], in0=mean_var[:, :, 1], scalar=EPS, in1=mean_sq[:], op0=ALU.add, op1=ALU.add
-        )
-        for k in range(2):
-            nc.gpsimd.tensor_tensor(out=root[k][:], in0=power[k][:], in1=minus_half[:], op=ALU.pow)
+        power = sb.tile([P, G], F32)
+        root = sb.tile([P, G], F32)
+        factor = sb.tile([P, G], F32)
 
-        def row_factor(k):
-            nc.vector.tensor_tensor(
-                out=factor[k][:], in0=root[k][:], in1=gain[:, 2 * k : 2 * k + 2], op=ALU.mult
+        def aggregate(k):
+            nc.vector.bn_aggr(out=mean_var[:, k, :], in_=stats[:, k, :, :].rearrange("p h s -> p (h s)"))
+
+        def power_from_moments(k):
+            nc.vector.tensor_scalar(
+                out=power[:, 2 + k : 3 + k],
+                in0=mean_var[:, k, 0:1],
+                scalar1=mean_var[:, k, 0:1],
+                scalar2=mean_var[:, k, 1:2],
+                op0=ALU.mult,
+                op1=ALU.add,
             )
 
+        def power_from_sums(k):
+            nc.vector.tensor_scalar(
+                out=power[:, k : k + 1],
+                in0=sums[1][:, k : k + 1],
+                scalar1=1.0 / N,
+                scalar2=first_part[:, k : k + 1],
+                op0=ALU.mult,
+                op1=ALU.add,
+            )
+
+        def inverse_root(g0, g1):
+            nc.gpsimd.tensor_tensor(
+                out=root[:, g0:g1], in0=power[:, g0:g1], in1=minus_half[:, 0 : g1 - g0], op=ALU.pow
+            )
+
+        def row_factor(g0, g1):
+            nc.vector.tensor_tensor(out=factor[:, g0:g1], in0=root[:, g0:g1], in1=gain[:, g0:g1], op=ALU.mult)
+
         h_raw = [sb.tile([P, PACK, HALF], BF16, name="h_raw%d" % h) for h in range(2)]
+        gate = [[sb.tile([P, HALF], F32, name="gate%d_%d" % (h, g)) for g in range(G)] for h in range(2)]
+
+        def sigmoid(h, g):
+            nc.scalar.activation(out=gate[h][g][:], in_=banks[h][g][:, gates], func=ACT.Sigmoid)
 
         def hidden(h, g):
-            gate = sb.tile([P, HALF], F32, name="gate%d_%d" % (h, g))
             hh = sb.tile([P, HALF], BF16, name="hh%d_%d" % (h, g))
-            nc.scalar.activation(out=gate[:], in_=banks[h][g][:, gates], func=ACT.Sigmoid)
             nc.vector.scalar_tensor_tensor(
                 out=hh[:],
                 in0=banks[h][g][:, values],
-                scalar=factor[g // 2][:, g % 2 : g % 2 + 1],
-                in1=gate[:],
+                scalar=factor[:, g : g + 1],
+                in1=gate[h][g][:],
                 op0=ALU.mult,
                 op1=ALU.mult,
             )
             nc.sync.dma_start(out=h_raw[h][ROWS * g : ROWS * (g + 1), :, :], in_=hh[:])
 
-        row_factor(0)
+        interleave(nc.vector.tensor_copy, w1q[0], w1_raw, 0, M)
+        nc.vector.transpose(out=cols[:], in_=rows[:])
+        nc.gpsimd.tensor_tensor(out=gain[:], in0=cols[:, 0:M:ROWS], in1=cols[:, M : 2 * M : ROWS], op=ALU.mult)
+        quantize(w1q)
+        shared_interleave(xq[0], x_raw[0], 144)
+        quantize(xq[0])
+        product(banks[0], w1q, xq[0], 0, (0, 2))
+        product(banks[0], w1q, xq[0], 0, (1, 3))
+        shared_interleave(xq[1], x_raw[1], 144)
+        quantize(xq[1])
+        product(banks[1], w1q, xq[1], 0, (0, 2))
+        product(banks[1], w1q, xq[1], 0, (1, 3))
+        interleave(nc.scalar.copy, w2q[0], w2_raw, 0, M // 2)
+        interleave(nc.vector.tensor_copy, w2q[0], w2_raw, M // 2, M)
+        sum_squares(0, 0)
+        moments(0, 0)
+        quantize(w2q)
+        sum_squares(0, 1)
+        moments(0, 1)
+        nc.gpsimd.tensor_scalar(
+            out=first_part[:], in0=sums[0][:], scalar1=1.0 / N, scalar2=EPS, op0=ALU.mult, op1=ALU.add
+        )
+        sum_squares(1, 0)
+        moments(1, 0)
+        nc.vector.tensor_scalar_add(out=stats[:, :, 0, 2], in0=stats[:, :, 0, 2], scalar1=N * EPS)
+        power_from_sums(0)
+        inverse_root(0, 1)
+        sum_squares(1, 1)
+        aggregate(0)
+        moments(1, 1)
+        power_from_moments(0)
+        power_from_sums(1)
+        inverse_root(1, 3)
+        aggregate(1)
+        row_factor(0, 1)
+        power_from_moments(1)
+        inverse_root(3, 4)
+
+        product(banks[0], w2q, xq[0], HALF, (0, 1))
+        product(banks[1], w2q, xq[1], HALF, (0,))
+        product(banks[0], w2q, xq[0], HALF, (2, 3))
+        product(banks[1], w2q, xq[1], HALF, (1, 2, 3))
+        steps = [(0, 0), (1, 0), (0, 1), (0, 2), (0, 3), (1, 1), (1, 2), (1, 3)]
+        for h, g in steps:
+            sigmoid(h, g)
         hidden(0, 0)
-        row_factor(1)
-        for g in range(1, G):
-            hidden(0, g)
-        for g in range(G):
-            hidden(1, g)
+        row_factor(1, 3)
+        hidden(1, 0)
+        hidden(0, 1)
+        row_factor(3, 4)
+        for h, g in steps[3:]:
+            hidden(h, g)
 
         out_rows = out.rearrange("g o n -> o g n")
 
@@ -206,15 +244,12 @@ def tile_rows_frownorm_kernel(tc, x, w1, w2, gn, hs, wo2, res, out):
             nc.sync.dma_start(out=out_rows[:, g, halves[h]], in_=y[:])
 
         interleave(nc.vector.tensor_copy, woq[0], wo_raw, 0, O)
-        shared_interleave(hq[0], h_raw[0], 176)
         quantize(woq)
-        quantize(hq[0])
-        product(banks[0], woq, hq[0], 0)
-        shared_interleave(hq[1], h_raw[1], 128)
-        finish(0, 0)
-        quantize(hq[1])
-        product(banks[1], woq, hq[1], 0)
-        for g in (2, 1, 3):
-            finish(0, g)
-        for g in (0, 2, 1, 3):
-            finish(1, g)
+        for h in range(2):
+            shared_interleave(hq[h], h_raw[h], 144)
+            quantize(hq[h])
+            product(banks[h], woq, hq[h], 0, (0, 1))
+            product(banks[h], woq, hq[h], 0, (2, 3))
+        for h in range(2):
+            for g in range(G):
+                finish(h, g)

@@ -136,16 +136,15 @@ def tile_rows_frownorm_kernel(tc, x, w1, w2, gn, hs, wo2, res, out):
             nc.vector.bn_aggr(out=mean_var[:, k, :], in_=stats[:, k, :, :].rearrange("p h s -> p (h s)"))
 
         def power_from_moments(k):
-            nc.vector.tensor_scalar(
+            nc.scalar.activation(
                 out=power[:, 2 + k : 3 + k],
-                in0=mean_var[:, k, 0:1],
-                scalar1=mean_var[:, k, 0:1],
-                scalar2=mean_var[:, k, 1:2],
-                op0=ALU.mult,
-                op1=ALU.add,
+                in_=mean_var[:, k, 0:1],
+                func=ACT.Identity,
+                scale=mean_var[:, k, 0:1],
+                bias=mean_var[:, k, 1:2],
             )
 
-        def power_from_sums(k):
+        def power_from_sums_vector(k):
             nc.vector.tensor_scalar(
                 out=power[:, k : k + 1],
                 in0=sums[1][:, k : k + 1],
@@ -155,13 +154,29 @@ def tile_rows_frownorm_kernel(tc, x, w1, w2, gn, hs, wo2, res, out):
                 op1=ALU.add,
             )
 
+        def power_from_sums_scalar(k):
+            nc.scalar.activation(
+                out=power[:, k : k + 1],
+                in_=sums[1][:, k : k + 1],
+                func=ACT.Identity,
+                scale=1.0 / N,
+                bias=first_part[:, k : k + 1],
+            )
+
         def inverse_root(g0, g1):
             nc.gpsimd.tensor_tensor(
                 out=root[:, g0:g1], in0=power[:, g0:g1], in1=minus_half[:, 0 : g1 - g0], op=ALU.pow
             )
 
-        def row_factor(g0, g1):
-            nc.vector.tensor_tensor(out=factor[:, g0:g1], in0=root[:, g0:g1], in1=gain[:, g0:g1], op=ALU.mult)
+        def row_factor_vector(g):
+            nc.vector.tensor_tensor(
+                out=factor[:, g : g + 1], in0=root[:, g : g + 1], in1=gain[:, g : g + 1], op=ALU.mult
+            )
+
+        def row_factor_scalar(g):
+            nc.scalar.activation(
+                out=factor[:, g : g + 1], in_=root[:, g : g + 1], func=ACT.Copy, scale=gain[:, g : g + 1]
+            )
 
         h_raw = [sb.tile([P, PACK, HALF], BF16, name="h_raw%d" % h) for h in range(2)]
         gate = [[sb.tile([P, HALF], F32, name="gate%d_%d" % (h, g)) for g in range(G)] for h in range(2)]
@@ -206,32 +221,34 @@ def tile_rows_frownorm_kernel(tc, x, w1, w2, gn, hs, wo2, res, out):
         sum_squares(1, 0)
         moments(1, 0)
         nc.vector.tensor_scalar_add(out=stats[:, :, 0, 2], in0=stats[:, :, 0, 2], scalar1=N * EPS)
-        power_from_sums(0)
+        power_from_sums_vector(0)
         inverse_root(0, 1)
         sum_squares(1, 1)
         aggregate(0)
         moments(1, 1)
-        power_from_moments(0)
-        power_from_sums(1)
-        inverse_root(1, 3)
         aggregate(1)
-        row_factor(0, 1)
-        power_from_moments(1)
-        inverse_root(3, 4)
 
         product(banks[0], w2q, xq[0], HALF, (0, 1))
         product(banks[1], w2q, xq[1], HALF, (0,))
         product(banks[0], w2q, xq[0], HALF, (2, 3))
         product(banks[1], w2q, xq[1], HALF, (1, 2, 3))
-        steps = [(0, 0), (1, 0), (0, 1), (0, 2), (0, 3), (1, 1), (1, 2), (1, 3)]
-        for h, g in steps:
-            sigmoid(h, g)
+        power_from_moments(0)
+        power_from_sums_scalar(1)
+        inverse_root(1, 3)
+        sigmoid(0, 0)
+        row_factor_scalar(0)
+        power_from_moments(1)
+        inverse_root(3, 4)
         hidden(0, 0)
-        row_factor(1, 3)
+        sigmoid(1, 0)
         hidden(1, 0)
+        sigmoid(0, 1)
+        row_factor_scalar(1)
+        row_factor_scalar(2)
         hidden(0, 1)
-        row_factor(3, 4)
-        for h, g in steps[3:]:
+        row_factor_vector(3)
+        for h, g in [(0, 2), (0, 3), (1, 1), (1, 2), (1, 3)]:
+            sigmoid(h, g)
             hidden(h, g)
 
         out_rows = out.rearrange("g o n -> o g n")

from contextlib import ExitStack

import concourse.mybir as mybir

G, D, M, O, N = 4, 128, 128, 128, 512
FLOPS = 3 * 2 * G * D * M * N

F32 = mybir.dt.float32
BF16 = mybir.dt.bfloat16
U32 = mybir.dt.uint32
U8 = mybir.dt.uint8
FP8X4 = mybir.dt.float8_e4m3fn_x4
ACT = mybir.ActivationFunctionType
ALU = mybir.AluOpType

P = 128
PACK = 4
ROWS = 32
HALF = N // 2
CALL = 128
EPS = 0.01


def tile_rows_frownorm_kernel(tc, x, w1, w2, gn, hs, wo2, res, out):
    nc = tc.nc

    def packed(ap):
        return ap.rearrange("g (p j) n -> (g p) j n", j=PACK)

    def interleave(copy, dst, src, c0, c1):
        copy(
            out=dst[:, c0:c1, :].rearrange("p (c i) j -> p c j i", i=4),
            in_=src[:, :, c0:c1].rearrange("p j (c i) -> p c j i", i=4),
        )

    with ExitStack() as ctx:
        sb = ctx.enter_context(tc.tile_pool(name="sb", bufs=1))
        ps = ctx.enter_context(tc.psum_pool(name="ps", bufs=1))
        ctx.enter_context(tc.manual_schedule())

        def operand(name, width):
            words = sb.tile([P, width, PACK], BF16, name=name + "_words", align_bytes=64)
            codes = sb.tile([P, width], U32, name=name + "_codes", align_bytes=64)
            scales = sb.tile([P, width], U8, name=name + "_scales", align_bytes=64)
            return words, codes, scales

        def quantize(op):
            words, codes, scales = op
            nc.vector.quantize_mx(
                out=codes[:].bitcast(FP8X4),
                scales=scales[:],
                in_=words[:].rearrange("p n j -> p (n j)"),
            )

        def product(banks, weights, moving, col0, groups):
            for c in range(0, HALF, CALL):
                for g in groups:
                    tile_rows = slice(ROWS * g, ROWS * (g + 1))
                    nc.tensor.matmul_mx(
                        out=banks[g][:, col0 + c : col0 + c + CALL],
                        lhsT=weights[1][tile_rows, :].bitcast(FP8X4),
                        lhsT_scale=weights[2][tile_rows, :],
                        rhs=moving[1][tile_rows, c : c + CALL].bitcast(FP8X4),
                        rhs_scale=moving[2][tile_rows, c : c + CALL],
                        start=True,
                        stop=True,
                    )

        halves = [slice(0, HALF), slice(HALF, N)]
        x_raw = [sb.tile([P, PACK, HALF], F32, name="x_raw%d" % h) for h in range(2)]
        w1_raw = sb.tile([P, PACK, M], F32)
        w2_raw = sb.tile([P, PACK, M], F32)
        wo_raw = sb.tile([P, PACK, O], F32)
        rows = sb.tile([P, 2 * M], F32, align_bytes=64)
        cols = sb.tile([P, 2 * M], F32, align_bytes=64)
        res_sb = sb.tile([P, G, N], F32)

        nc.sync.dma_start(out=w1_raw[:], in_=packed(w1))
        nc.gpsimd.memset(rows[:], 0.0)
        for k, vec in enumerate((gn, hs)):
            nc.sync.dma_start(
                out=rows[0:P:ROWS, k * M : (k + 1) * M].rearrange("q (g c) -> q g c", g=G),
                in_=vec.rearrange("g (q c) o -> q g (c o)", c=ROWS),
            )
        nc.sync.dma_start(out=x_raw[0][:], in_=packed(x)[:, :, halves[0]])
        nc.sync.dma_start(out=x_raw[1][:], in_=packed(x)[:, :, halves[1]])
        nc.sync.dma_start(out=w2_raw[:], in_=packed(w2))
        nc.sync.dma_start(out=wo_raw[:], in_=packed(wo2))
        nc.sync.dma_start(out=res_sb[:], in_=res.rearrange("g o n -> o g n"))

        minus_half = sb.tile([P, 2], F32)
        ones = sb.tile([P, 2], F32)
        warm = sb.tile([P, 2], F32)
        warm_pow = sb.tile([P, 2], F32)
        nc.gpsimd.memset(minus_half[:], -0.5)
        nc.gpsimd.memset(ones[:], 1.0)
        nc.gpsimd.tensor_tensor(out=warm_pow[:], in0=ones[:], in1=minus_half[:], op=ALU.pow)
        nc.scalar.activation(out=warm[:], in_=minus_half[:], func=ACT.Sigmoid)

        xq = [operand("x%d" % h, HALF) for h in range(2)]
        w1q = operand("w1", M)
        w2q = operand("w2", M)
        woq = operand("wo", O)
        hq = [operand("h%d" % h, HALF) for h in range(2)]
        banks = [[ps.tile([P, N], F32, name="bank%d_%d" % (h, g)) for g in range(G)] for h in range(2)]
        values = slice(0, HALF)
        gates = slice(HALF, N)

        def shared_interleave(op, raw, split):
            interleave(nc.vector.tensor_copy, op[0], raw, 0, split)
            interleave(nc.scalar.copy, op[0], raw, split, HALF)

        squares = sb.tile([P, 2, 2, HALF], BF16)
        sums = [sb.tile([P, 2], F32, name="sums%d" % h) for h in range(2)]
        stats = sb.tile([P, 2, 2, 6], F32)

        def sum_squares(h, k):
            nc.scalar.activation(
                out=squares[:, h, k, :],
                in_=banks[h][k][:, values],
                func=ACT.Square,
                accum_out=sums[h][:, k : k + 1],
            )

        def moments(h, k):
            nc.vector.bn_stats(out=stats[:, k, h, :], in_=banks[h][2 + k][:, values])

        gain = sb.tile([P, G], F32)
        first_part = sb.tile([P, 2], F32)
        mean_var = sb.tile([P, 2, 2], F32)
        power = sb.tile([P, G], F32)
        root = sb.tile([P, G], F32)
        factor = sb.tile([P, G], F32)

        def aggregate(k):
            nc.vector.bn_aggr(out=mean_var[:, k, :], in_=stats[:, k, :, :].rearrange("p h s -> p (h s)"))

        def power_from_moments(k):
            nc.scalar.activation(
                out=power[:, 2 + k : 3 + k],
                in_=mean_var[:, k, 0:1],
                func=ACT.Identity,
                scale=mean_var[:, k, 0:1],
                bias=mean_var[:, k, 1:2],
            )

        def power_from_sums_vector(k):
            nc.vector.tensor_scalar(
                out=power[:, k : k + 1],
                in0=sums[1][:, k : k + 1],
                scalar1=1.0 / N,
                scalar2=first_part[:, k : k + 1],
                op0=ALU.mult,
                op1=ALU.add,
            )

        def power_from_sums_scalar(k):
            nc.scalar.activation(
                out=power[:, k : k + 1],
                in_=sums[1][:, k : k + 1],
                func=ACT.Identity,
                scale=1.0 / N,
                bias=first_part[:, k : k + 1],
            )

        def inverse_root(g0, g1):
            nc.gpsimd.tensor_tensor(
                out=root[:, g0:g1], in0=power[:, g0:g1], in1=minus_half[:, 0 : g1 - g0], op=ALU.pow
            )

        def row_factor_vector(g):
            nc.vector.tensor_tensor(
                out=factor[:, g : g + 1], in0=root[:, g : g + 1], in1=gain[:, g : g + 1], op=ALU.mult
            )

        def row_factor_scalar(g):
            nc.scalar.activation(
                out=factor[:, g : g + 1], in_=root[:, g : g + 1], func=ACT.Copy, scale=gain[:, g : g + 1]
            )

        h_raw = [sb.tile([P, PACK, HALF], BF16, name="h_raw%d" % h) for h in range(2)]
        gate = [[sb.tile([P, HALF], F32, name="gate%d_%d" % (h, g)) for g in range(G)] for h in range(2)]

        def sigmoid(h, g):
            nc.scalar.activation(out=gate[h][g][:], in_=banks[h][g][:, gates], func=ACT.Sigmoid)

        def hidden(h, g):
            hh = sb.tile([P, HALF], BF16, name="hh%d_%d" % (h, g))
            nc.vector.scalar_tensor_tensor(
                out=hh[:],
                in0=banks[h][g][:, values],
                scalar=factor[:, g : g + 1],
                in1=gate[h][g][:],
                op0=ALU.mult,
                op1=ALU.mult,
            )
            nc.sync.dma_start(out=h_raw[h][ROWS * g : ROWS * (g + 1), :, :], in_=hh[:])

        interleave(nc.vector.tensor_copy, w1q[0], w1_raw, 0, M)
        nc.vector.transpose(out=cols[:], in_=rows[:])
        nc.gpsimd.tensor_tensor(out=gain[:], in0=cols[:, 0:M:ROWS], in1=cols[:, M : 2 * M : ROWS], op=ALU.mult)
        quantize(w1q)
        shared_interleave(xq[0], x_raw[0], 144)
        quantize(xq[0])
        product(banks[0], w1q, xq[0], 0, (0, 2))
        product(banks[0], w1q, xq[0], 0, (1, 3))
        shared_interleave(xq[1], x_raw[1], 144)
        quantize(xq[1])
        product(banks[1], w1q, xq[1], 0, (0, 2))
        product(banks[1], w1q, xq[1], 0, (1, 3))
        interleave(nc.scalar.copy, w2q[0], w2_raw, 0, M // 2)
        interleave(nc.vector.tensor_copy, w2q[0], w2_raw, M // 2, M)
        sum_squares(0, 0)
        moments(0, 0)
        quantize(w2q)
        sum_squares(0, 1)
        moments(0, 1)
        nc.gpsimd.tensor_scalar(
            out=first_part[:], in0=sums[0][:], scalar1=1.0 / N, scalar2=EPS, op0=ALU.mult, op1=ALU.add
        )
        sum_squares(1, 0)
        moments(1, 0)
        nc.vector.tensor_scalar_add(out=stats[:, :, 0, 2], in0=stats[:, :, 0, 2], scalar1=N * EPS)
        power_from_sums_vector(0)
        inverse_root(0, 1)
        sum_squares(1, 1)
        aggregate(0)
        moments(1, 1)
        aggregate(1)

        product(banks[0], w2q, xq[0], HALF, (0, 1))
        product(banks[1], w2q, xq[1], HALF, (0,))
        product(banks[0], w2q, xq[0], HALF, (2, 3))
        product(banks[1], w2q, xq[1], HALF, (1, 2, 3))
        power_from_moments(0)
        power_from_sums_scalar(1)
        inverse_root(1, 3)
        sigmoid(0, 0)
        row_factor_scalar(0)
        power_from_moments(1)
        inverse_root(3, 4)
        hidden(0, 0)
        sigmoid(1, 0)
        hidden(1, 0)
        sigmoid(0, 1)
        row_factor_scalar(1)
        row_factor_scalar(2)
        hidden(0, 1)
        row_factor_vector(3)
        for h, g in [(0, 2), (0, 3), (1, 1), (1, 2), (1, 3)]:
            sigmoid(h, g)
            hidden(h, g)

        out_rows = out.rearrange("g o n -> o g n")

        def finish(h, g):
            y = sb.tile([P, HALF], F32, name="y%d_%d" % (h, g))
            nc.vector.tensor_tensor(
                out=y[:], in0=banks[h][g][:, values], in1=res_sb[:, g, halves[h]], op=ALU.add
            )
            nc.sync.dma_start(out=out_rows[:, g, halves[h]], in_=y[:])

        interleave(nc.vector.tensor_copy, woq[0], wo_raw, 0, O)
        quantize(woq)
        for h in range(2):
            shared_interleave(hq[h], h_raw[h], 144)
            quantize(hq[h])
            product(banks[h], woq, hq[h], 0, (0, 1))
            product(banks[h], woq, hq[h], 0, (2, 3))
        for h in range(2):
            for g in range(G):
                finish(h, g)
